import numpy as np
import ml_dtypes


def mxq(x, axis, fmt="e4m3"):
    dtype, down = {"e4m3": (ml_dtypes.float8_e4m3fn, 7), "e5m2": (ml_dtypes.float8_e5m2, 14)}[fmt]
    v = np.moveaxis(np.asarray(x, np.float32).astype(ml_dtypes.bfloat16).astype(np.float64), axis, -1)
    blocks = v.reshape(v.shape[:-1] + (-1, 32))
    amax = np.abs(blocks).max(-1, keepdims=True)
    byte = np.maximum(np.where(amax > 0, np.frexp(amax)[1] - 1 + 127, 0) - down, 1)
    scale = np.exp2(byte - 127.0)
    codes = (blocks / scale).astype(np.float32).astype(dtype).astype(np.float64)
    return np.moveaxis((codes * scale).reshape(v.shape), -1, axis)


WIDE = False


def mx_kscale(k):
    if not WIDE:
        return np.ones(k)
    levels = np.array([10, -10, 5, -5, 0])
    if k % 512:
        return np.exp2(np.random.permutation(np.resize(levels, k // 32))).repeat(32)
    a = np.empty((k // 512, 16))
    for p in range(k // 512):
        a[p, :8] = np.random.permutation(np.resize(levels, 8))
        for g in range(8):
            far = levels[np.abs(levels - a[p, g]) >= 10]
            a[p, g + 8] = far[np.random.randint(len(far))]
    return np.exp2(a.ravel()).repeat(32)


def f64(x):
    return np.asarray(x).astype(np.float64)


def striped(idx):
    return np.tile(idx.reshape(-1, 16).T, (8, 1)).astype(np.uint16)


def unstriped(offs):
    return offs[:16].T.reshape(-1).astype(np.int64)


E2M1 = np.array([0.0, 0.5, 1.0, 1.5, 2.0, 3.0, 4.0, 6.0, -0.0, -0.5, -1.0, -1.5, -2.0, -3.0, -4.0, -6.0])


def pack_weight(w, fmt):
    k, n = w.shape
    w = f64(np.asarray(w, np.float32).astype(ml_dtypes.bfloat16)).reshape(k // 32, 32, n)
    amax = np.abs(w).max(1)
    if fmt == "e4m3":
        byte = np.frexp(amax)[1] - 1 + 127 - 7
    else:
        mant, ex = np.frexp(amax / 6.0)
        byte = np.where(mant > 0.5, ex, ex - 1) + 127
    byte = np.clip(np.where(amax > 0, byte, 1), 1, 254)
    scaled = (w * np.exp2(127.0 - byte)[:, None, :]).reshape(k, n).astype(np.float32)
    by_word = np.ascontiguousarray(scaled.reshape(k // 512, 128, 4, n).transpose(0, 1, 3, 2))
    if fmt == "e4m3":
        words = by_word.astype(ml_dtypes.float8_e4m3fn).view(np.uint8)
    else:
        c = by_word.astype(ml_dtypes.float4_e2m1fn).view(np.uint8) & 0xF
        words = (c[..., 0::2] | (c[..., 1::2] << 4)).reshape(k // 512, 128, 2 * n)
    return np.ascontiguousarray(words), np.ascontiguousarray(byte.astype(np.uint8).reshape(k // 512, 16, n))


def unpack_weight(words, scales, fmt):
    g, _, n = scales.shape
    words = np.ascontiguousarray(words).reshape(g, 128, n, -1)
    if fmt == "e4m3":
        vals = words.view(ml_dtypes.float8_e4m3fn).astype(np.float64)
    else:
        nib = np.empty((g, 128, n, 4), np.uint8)
        nib[..., 0::2] = words & 0xF
        nib[..., 1::2] = words >> 4
        vals = E2M1[nib]
    vals = vals * np.repeat(np.exp2(scales.astype(np.float64) - 127.0), 8, axis=1)[..., None]
    return vals.transpose(0, 1, 3, 2).reshape(g * 512, n)


def relu(v):
    return np.maximum(v, 0.0)


K, T, E, C, N = 2048, 512, 4, 256, 128


def by_expert(wq, xq):
    return np.concatenate([wq[e].T @ xq[:, e * C:(e + 1) * C] for e in range(E)], axis=1)


def setup_inputs():
    n = np.random.standard_normal
    s = mx_kscale(K)[:, None]
    first = np.random.permutation(np.repeat(np.arange(E), T // E))
    second = (first + 1 + np.random.permutation(np.repeat(np.arange(E - 1), -(-T // (E - 1)))[:T])) % E
    while np.bincount(second, minlength=E).max() != T // E:
        load = np.bincount(second, minlength=E); hi, lo = int(load.argmax()), int(load.argmin())
        t = np.flatnonzero((second == hi) & (first != lo))[0]; second[t] = lo
    slot_token = np.empty(E * C, np.int64); pos = np.empty((2, T), np.int64); fill = np.zeros(E, np.int64)
    place = np.stack([np.random.permutation(C) for _ in range(E)])
    for r, deal in enumerate((first, second)):
        for t in np.random.permutation(T):
            e = deal[t]; j = e * C + place[e, fill[e]]; fill[e] += 1; slot_token[j] = t; pos[r, t] = j
    g = np.random.uniform(0.2, 0.8, T)
    w = [pack_weight(m, "e2m1") for m in n((E + 1, K, N)) / np.sqrt(K) / s[None]]
    return {
        "xT": (n((K, T)) * s).astype(np.float32),
        "w_words": np.stack([m[0] for m in w]),
        "w_scales": np.stack([m[1] for m in w]),
        "b": (0.3 * n((N, E + 1))).astype(np.float32),
        "gate": np.stack([np.tile(g, (N, 1)), np.tile(1.0 - g, (N, 1))]).astype(np.float32),
        "offs": striped(slot_token),
        "pos1": striped(pos[0]),
        "pos2": striped(pos[1]),
    }


def reference(xT, w_words, w_scales, b, gate, offs, pos1, pos2):
    idx = unstriped(offs)
    w = np.stack([unpack_weight(w_words[e], w_scales[e], "e2m1") for e in range(E + 1)])
    wq = w
    xs = mxq(f64(xT), 0, "e4m3")
    ys = relu((wq[E].T @ xs) + f64(b)[:, E:])
    xq = mxq(f64(xT)[:, idx], 0, "e4m3")
    y = by_expert(w, xq)
    y = relu(y + np.repeat(f64(b)[:, :E], C, axis=1))
    return ys + f64(gate[0]) * y[:, unstriped(pos1)] + f64(gate[1]) * y[:, unstriped(pos2)]

@@ -1,0 +1,154 @@
+from contextlib import ExitStack
+
+import concourse.mybir as mybir
+
+F32 = mybir.dt.float32
+BF16 = mybir.dt.bfloat16
+U32 = mybir.dt.uint32
+I32 = mybir.dt.int32
+U16 = mybir.dt.uint16
+U8 = mybir.dt.uint8
+FP8X4 = mybir.dt.float8_e4m3fn_x4
+FP4X4 = mybir.dt.float4_e2m1fn_x4
+RELU = mybir.ActivationFunctionType.Relu
+MULT = mybir.AluOpType.mult
+
+P = 128
+K, T, E, C, N = 2048, 512, 4, 256, 128
+K_PASS = 512
+PASSES = K // K_PASS
+SLOTS = E * C
+
+FLOPS = 2 * K * N * (SLOTS + T)
+
+
+def tile_moe_shr_lin_relu_kernel(tc, xT, w_words, w_scales, b, gate, offs, pos1, pos2, out):
+    nc = tc.nc
+    with ExitStack() as ctx:
+        keep = ctx.enter_context(tc.tile_pool(name="keep", bufs=1))
+        psum = ctx.enter_context(tc.psum_pool(name="psum", bufs=1))
+
+        offs_sb = keep.tile([P, SLOTS // 16], U16, name="offs_sb")
+        pos1_sb = keep.tile([P, T // 16], U16, name="pos1_sb")
+        pos2_sb = keep.tile([P, T // 16], U16, name="pos2_sb")
+        w_sb = keep.tile([P, (E + 1) * PASSES, 2 * N], U8, name="w_sb", align_bytes=64)
+        ws_sb = keep.tile([P, (E + 1) * PASSES, N], U8, name="ws_sb", align_bytes=64)
+        b_sb = keep.tile([P, E + 1], F32, name="b_sb")
+        gate_sb = keep.tile([P, 2, T], F32, name="gate_sb")
+        y_sb = keep.tile([P, SLOTS], F32, name="y_sb")
+        ys_sb = keep.tile([P, T], F32, name="ys_sb")
+
+        nc.vector.memset(ws_sb[:].rearrange("p g n -> p (g n)").bitcast(I32), 0)
+
+        nc.sync.dma_start(offs_sb[:], offs)
+        raw = {}
+        for a in range(PASSES):
+            rows = xT[a * K_PASS : (a + 1) * K_PASS, :].rearrange("(p u e) w -> u p e w", u=2, e=2)
+            for u in range(2):
+                raw[a, u] = keep.tile([P, 2, T], F32, name=f"raw_{a}_{u}")
+                nc.sync.dma_start(raw[a, u][:], rows[u])
+        nc.sync.dma_start(w_sb[:].bitcast(I32), w_words.rearrange("e a p n -> p (e a) n").bitcast(I32))
+        scale_rows = w_scales.rearrange("e a q n -> q (e a) n").bitcast(I32)
+        for quad in range(4):
+            nc.sync.dma_start(ws_sb[32 * quad : 32 * quad + 4].bitcast(I32), scale_rows[4 * quad : 4 * quad + 4])
+        nc.sync.dma_start(b_sb[:], b)
+        nc.sync.dma_start(pos1_sb[:], pos1)
+        nc.sync.dma_start(pos2_sb[:], pos2)
+        nc.sync.dma_start(gate_sb[:], gate.rearrange("r n t -> n r t"))
+
+        pairs = {}
+
+        def cast(a, u):
+            if u == 0:
+                pairs[a] = keep.tile([P, 2, T, 2], BF16, name=f"pairs_{a}", align_bytes=64)
+            src = raw[a, u][:].rearrange("p e w -> p w e")
+            if a == 0 and u == 0:
+                nc.vector.tensor_copy(pairs[a][:, u], src)
+            else:
+                nc.scalar.copy(pairs[a][:, u], src)
+
+        banks = [psum.tile([P, N], F32, name=f"bank{i}", tag=f"bank{i}") for i in range(8)]
+        codes = {}
+        scales = {}
+        gath = {}
+
+        def gather(a, e, u):
+            if u == 0:
+                gath[a, e] = keep.tile([P, 2, C, 2], BF16, name=f"gath_{a}_{e}", align_bytes=64)
+            nc.vector.tensor_copy(
+                gath[a, e][:, u].rearrange("p n e -> p (n e)").bitcast(U32),
+                pairs[a][:, u].rearrange("p w e -> p (w e)").bitcast(U32).indirect(offs_sb[:, e * C // 16 : (e + 1) * C // 16]),
+            )
+
+        def quantize(a, e):
+            q_in = keep.tile([P, C, 2, 2], BF16, name=f"q_in_{a}_{e}", align_bytes=64)
+            nc.scalar.copy(q_in[:], gath[a, e][:].rearrange("p u n e -> p n u e"))
+            codes[a, e] = keep.tile([P, C], U32, name=f"codes_{a}_{e}", align_bytes=64)
+            scales[a, e] = keep.tile([P, C], U8, name=f"scales_{a}_{e}", align_bytes=64)
+            nc.vector.quantize_mx(out=codes[a, e][:].bitcast(FP8X4), scales=scales[a, e][:], in_=q_in[:].rearrange("p n u e -> p (n u e)"))
+
+        def multiply(a, e):
+            for h in range(2):
+                cols = slice(h * N, (h + 1) * N)
+                nc.tensor.matmul_mx(
+                    out=banks[2 * e + h][:],
+                    lhsT=w_sb[:, e * PASSES + a, :].bitcast(FP4X4),
+                    lhsT_scale=ws_sb[:, e * PASSES + a, :],
+                    rhs=codes[a, e][:, cols].bitcast(FP8X4),
+                    rhs_scale=scales[a, e][:, cols],
+                    start=(a == 0),
+                    stop=(a == PASSES - 1),
+                )
+
+        cast(0, 0)
+        cast(0, 1)
+        for a in range(PASSES):
+            if a + 1 < PASSES:
+                cast(a + 1, 0)
+                cast(a + 1, 1)
+            if a == 0:
+                for e in range(E):
+                    gather(a, e, 0)
+            for e in range(E):
+                if a != 0:
+                    gather(a, e, 0)
+                gather(a, e, 1)
+                quantize(a, e)
+                multiply(a, e)
+                if a == PASSES - 1:
+                    for h in range(2):
+                        nc.scalar.activation(
+                            y_sb[:, e * C + h * N : e * C + (h + 1) * N], banks[2 * e + h][:], RELU, bias=b_sb[:, e : e + 1]
+                        )
+
+        shared = psum.tile([P, T], F32, name="shared", tag="bank0")
+        for a in range(PASSES):
+            q_in = keep.tile([P, T, 2, 2], BF16, name=f"q_shared_{a}", align_bytes=64)
+            nc.vector.tensor_copy(q_in[:], pairs[a][:].rearrange("p u w e -> p w u e"))
+            s_codes = keep.tile([P, T], U32, name=f"s_codes_{a}", align_bytes=64)
+            s_scales = keep.tile([P, T], U8, name=f"s_scales_{a}", align_bytes=64)
+            nc.vector.quantize_mx(out=s_codes[:].bitcast(FP8X4), scales=s_scales[:], in_=q_in[:].rearrange("p n u e -> p (n u e)"))
+            nc.tensor.matmul_mx(
+                out=shared[:],
+                lhsT=w_sb[:, E * PASSES + a, :].bitcast(FP4X4),
+                lhsT_scale=ws_sb[:, E * PASSES + a, :],
+                rhs=s_codes[:].bitcast(FP8X4),
+                rhs_scale=s_scales[:],
+                start=(a == 0),
+                stop=(a == PASSES - 1),
+            )
+        nc.scalar.activation(ys_sb[:], shared[:], RELU, bias=b_sb[:, E : E + 1])
+
+        half = T // 2
+        for h in range(2):
+            cols = slice(h * half, (h + 1) * half)
+            lst = slice(h * half // 16, (h + 1) * half // 16)
+            first = keep.tile([P, half], F32, name=f"first_{h}")
+            second = keep.tile([P, half], F32, name=f"second_{h}")
+            nc.vector.tensor_tensor(first[:], y_sb[:].indirect(pos1_sb[:, lst]), gate_sb[:, 0, cols], MULT)
+            nc.vector.tensor_tensor(second[:], y_sb[:].indirect(pos2_sb[:, lst]), gate_sb[:, 1, cols], MULT)
+            partial = keep.tile([P, half], F32, name=f"partial_{h}")
+            total = keep.tile([P, half], F32, name=f"total_{h}")
+            nc.vector.tensor_add(partial[:], first[:], ys_sb[:, cols])
+            nc.vector.tensor_add(total[:], partial[:], second[:])
+            nc.sync.dma_start(out[:, cols], total[:])

@@ -11,7 +11,9 @@ U8 = mybir.dt.uint8
 FP8X4 = mybir.dt.float8_e4m3fn_x4
 FP4X4 = mybir.dt.float4_e2m1fn_x4
 RELU = mybir.ActivationFunctionType.Relu
+COPY = mybir.ActivationFunctionType.Copy
 MULT = mybir.AluOpType.mult
+ADD = mybir.AluOpType.add
 
 P = 128
 K, T, E, C, N = 2048, 512, 4, 256, 128
@@ -44,9 +46,9 @@ def tile_moe_shr_lin_relu_kernel(tc, xT, w_words, w_scales, b, gate, offs, pos1,
         raw = {}
         for a in range(PASSES):
             rows = xT[a * K_PASS : (a + 1) * K_PASS, :].rearrange("(p u e) w -> u p e w", u=2, e=2)
+            raw[a] = keep.tile([P, 4, T], F32, name=f"raw_{a}")
             for u in range(2):
-                raw[a, u] = keep.tile([P, 2, T], F32, name=f"raw_{a}_{u}")
-                nc.sync.dma_start(raw[a, u][:], rows[u])
+                nc.sync.dma_start(raw[a][:, 2 * u : 2 * u + 2], rows[u])
         nc.sync.dma_start(w_sb[:].bitcast(I32), w_words.rearrange("e a p n -> p (e a) n").bitcast(I32))
         scale_rows = w_scales.rearrange("e a q n -> q (e a) n").bitcast(I32)
         for quad in range(4):
@@ -58,10 +60,15 @@ def tile_moe_shr_lin_relu_kernel(tc, xT, w_words, w_scales, b, gate, offs, pos1,
 
         pairs = {}
 
+        planes = keep.tile([P, 4, T], BF16, name="planes", align_bytes=64)
+
         def cast(a, u):
+            if a == PASSES - 1:
+                nc.scalar.copy(planes[:, 2 * u : 2 * u + 2], raw[a][:, 2 * u : 2 * u + 2])
+                return
             if u == 0:
                 pairs[a] = keep.tile([P, 2, T, 2], BF16, name=f"pairs_{a}", align_bytes=64)
-            src = raw[a, u][:].rearrange("p e w -> p w e")
+            src = raw[a][:, 2 * u : 2 * u + 2].rearrange("p e w -> p w e")
             if a == 0 and u == 0:
                 nc.vector.tensor_copy(pairs[a][:, u], src)
             else:
@@ -70,32 +77,39 @@ def tile_moe_shr_lin_relu_kernel(tc, xT, w_words, w_scales, b, gate, offs, pos1,
         banks = [psum.tile([P, N], F32, name=f"bank{i}", tag=f"bank{i}") for i in range(8)]
         codes = {}
         scales = {}
-        gath = {}
+        def new_codes(a):
+            codes[a] = keep.tile([P, SLOTS], U32, name=f"codes_{a}", align_bytes=64)
+            scales[a] = keep.tile([P, SLOTS], U8, name=f"scales_{a}", align_bytes=64)
 
-        def gather(a, e, u):
-            if u == 0:
-                gath[a, e] = keep.tile([P, 2, C, 2], BF16, name=f"gath_{a}_{e}", align_bytes=64)
-            nc.vector.tensor_copy(
-                gath[a, e][:, u].rearrange("p n e -> p (n e)").bitcast(U32),
-                pairs[a][:, u].rearrange("p w e -> p (w e)").bitcast(U32).indirect(offs_sb[:, e * C // 16 : (e + 1) * C // 16]),
-            )
+        def vector_pass(a):
+            gath = keep.tile([P, 2, SLOTS, 2], BF16, name=f"gath_{a}", align_bytes=64)
+            q_in = keep.tile([P, SLOTS, 2, 2], BF16, name=f"q_in_{a}", align_bytes=64)
+            new_codes(a)
+            for u in range(2):
+                for lo, hi in ((0, 384), (384, 768), (768, 1024)):
+                    nc.vector.tensor_copy(
+                        gath[:, u, lo:hi].rearrange("p n e -> p (n e)").bitcast(U32),
+                        pairs[a][:, u].rearrange("p w e -> p (w e)").bitcast(U32).indirect(offs_sb[:, lo // 16 : hi // 16]),
+                    )
+            nc.vector.tensor_copy(q_in[:], gath[:].rearrange("p u n e -> p n u e"))
+            nc.vector.quantize_mx(out=codes[a][:].bitcast(FP8X4), scales=scales[a][:], in_=q_in[:].rearrange("p n u e -> p (n u e)"))
 
-        def quantize(a, e):
-            q_in = keep.tile([P, C, 2, 2], BF16, name=f"q_in_{a}_{e}", align_bytes=64)
-            nc.scalar.copy(q_in[:], gath[a, e][:].rearrange("p u n e -> p n u e"))
-            codes[a, e] = keep.tile([P, C], U32, name=f"codes_{a}_{e}", align_bytes=64)
-            scales[a, e] = keep.tile([P, C], U8, name=f"scales_{a}_{e}", align_bytes=64)
-            nc.vector.quantize_mx(out=codes[a, e][:].bitcast(FP8X4), scales=scales[a, e][:], in_=q_in[:].rearrange("p n u e -> p (n u e)"))
+        def scalar_chunk(a, e):
+            q_in = keep.tile([P, C, 4], BF16, name=f"q_in_{a}_{e}", align_bytes=64)
+            for t in range(4):
+                nc.scalar.activation(q_in[:, :, t], planes[:, t].indirect(offs_sb[:, e * C // 16 : (e + 1) * C // 16]), COPY)
+            cols = slice(e * C, (e + 1) * C)
+            nc.vector.quantize_mx(out=codes[a][:, cols].bitcast(FP8X4), scales=scales[a][:, cols], in_=q_in[:].rearrange("p n t -> p (n t)"))
 
         def multiply(a, e):
             for h in range(2):
-                cols = slice(h * N, (h + 1) * N)
+                cols = slice(e * C + h * N, e * C + (h + 1) * N)
                 nc.tensor.matmul_mx(
                     out=banks[2 * e + h][:],
                     lhsT=w_sb[:, e * PASSES + a, :].bitcast(FP4X4),
                     lhsT_scale=ws_sb[:, e * PASSES + a, :],
-                    rhs=codes[a, e][:, cols].bitcast(FP8X4),
-                    rhs_scale=scales[a, e][:, cols],
+                    rhs=codes[a][:, cols].bitcast(FP8X4),
+                    rhs_scale=scales[a][:, cols],
                     start=(a == 0),
                     stop=(a == PASSES - 1),
                 )
@@ -106,14 +120,13 @@ def tile_moe_shr_lin_relu_kernel(tc, xT, w_words, w_scales, b, gate, offs, pos1,
             if a + 1 < PASSES:
                 cast(a + 1, 0)
                 cast(a + 1, 1)
-            if a == 0:
-                for e in range(E):
-                    gather(a, e, 0)
+            if a < PASSES - 1:
+                vector_pass(a)
+            else:
+                new_codes(a)
             for e in range(E):
-                if a != 0:
-                    gather(a, e, 0)
-                gather(a, e, 1)
-                quantize(a, e)
+                if a == PASSES - 1:
+                    scalar_chunk(a, e)
                 multiply(a, e)
                 if a == PASSES - 1:
                     for h in range(2):
@@ -123,11 +136,14 @@ def tile_moe_shr_lin_relu_kernel(tc, xT, w_words, w_scales, b, gate, offs, pos1,
 
         shared = psum.tile([P, T], F32, name="shared", tag="bank0")
         for a in range(PASSES):
-            q_in = keep.tile([P, T, 2, 2], BF16, name=f"q_shared_{a}", align_bytes=64)
-            nc.vector.tensor_copy(q_in[:], pairs[a][:].rearrange("p u w e -> p w u e"))
+            q_in = keep.tile([P, T, 4], BF16, name=f"q_shared_{a}", align_bytes=64)
+            for lo in range(0, T, 64):
+                nc.gpsimd.tensor_scalar(
+                    q_in[:, lo : lo + 64], raw[a][:, :, lo : lo + 64].rearrange("p t w -> p w t"), 1.0, 0.0, MULT, ADD
+                )
             s_codes = keep.tile([P, T], U32, name=f"s_codes_{a}", align_bytes=64)
             s_scales = keep.tile([P, T], U8, name=f"s_scales_{a}", align_bytes=64)
-            nc.vector.quantize_mx(out=s_codes[:].bitcast(FP8X4), scales=s_scales[:], in_=q_in[:].rearrange("p n u e -> p (n u e)"))
+            nc.vector.quantize_mx(out=s_codes[:].bitcast(FP8X4), scales=s_scales[:], in_=q_in[:].rearrange("p n t -> p (n t)"))
             nc.tensor.matmul_mx(
                 out=shared[:],
                 lhsT=w_sb[:, E * PASSES + a, :].bitcast(FP4X4),

@@ -13,13 +13,14 @@ FP4X4 = mybir.dt.float4_e2m1fn_x4
 RELU = mybir.ActivationFunctionType.Relu
 COPY = mybir.ActivationFunctionType.Copy
 MULT = mybir.AluOpType.mult
-ADD = mybir.AluOpType.add
 
 P = 128
 K, T, E, C, N = 2048, 512, 4, 256, 128
 K_PASS = 512
 PASSES = K // K_PASS
+LAST = PASSES - 1
 SLOTS = E * C
+PIECES = ((0, 384), (384, 768), (768, 1024))
 
 FLOPS = 2 * K * N * (SLOTS + T)
 
@@ -39,14 +40,23 @@ def tile_moe_shr_lin_relu_kernel(tc, xT, w_words, w_scales, b, gate, offs, pos1,
         gate_sb = keep.tile([P, 2, T], F32, name="gate_sb")
         y_sb = keep.tile([P, SLOTS], F32, name="y_sb")
         ys_sb = keep.tile([P, T], F32, name="ys_sb")
+        planes = keep.tile([P, 4, T], BF16, name="planes", align_bytes=64)
+        banks = [psum.tile([P, N], F32, name=f"bank{i}", tag=f"bank{i}") for i in range(8)]
+        raw, pairs, gath, q_in, codes, scales = {}, {}, {}, {}, {}, {}
+        for a in range(PASSES):
+            raw[a] = keep.tile([P, 4, T], F32, name=f"raw_{a}")
+            codes[a] = keep.tile([P, SLOTS], U32, name=f"codes_{a}", align_bytes=64)
+            scales[a] = keep.tile([P, SLOTS], U8, name=f"scales_{a}", align_bytes=64)
+            q_in[a] = keep.tile([P, SLOTS, 4], BF16, name=f"q_in_{a}", align_bytes=64)
+            if a != LAST:
+                pairs[a] = keep.tile([P, 2, T, 2], BF16, name=f"pairs_{a}", align_bytes=64)
+                gath[a] = keep.tile([P, 2, SLOTS, 2], BF16, name=f"gath_{a}", align_bytes=64)
 
         nc.vector.memset(ws_sb[:].rearrange("p g n -> p (g n)").bitcast(I32), 0)
 
         nc.sync.dma_start(offs_sb[:], offs)
-        raw = {}
         for a in range(PASSES):
             rows = xT[a * K_PASS : (a + 1) * K_PASS, :].rearrange("(p u e) w -> u p e w", u=2, e=2)
-            raw[a] = keep.tile([P, 4, T], F32, name=f"raw_{a}")
             for u in range(2):
                 nc.sync.dma_start(raw[a][:, 2 * u : 2 * u + 2], rows[u])
         nc.sync.dma_start(w_sb[:].bitcast(I32), w_words.rearrange("e a p n -> p (e a) n").bitcast(I32))
@@ -58,48 +68,35 @@ def tile_moe_shr_lin_relu_kernel(tc, xT, w_words, w_scales, b, gate, offs, pos1,
         nc.sync.dma_start(pos2_sb[:], pos2)
         nc.sync.dma_start(gate_sb[:], gate.rearrange("r n t -> n r t"))
 
-        pairs = {}
+        def cast(a, u, lo, hi, copy):
+            copy(pairs[a][:, u, lo:hi], raw[a][:, 2 * u : 2 * u + 2, lo:hi].rearrange("p e w -> p w e"))
 
-        planes = keep.tile([P, 4, T], BF16, name="planes", align_bytes=64)
+        def gather(a, i):
+            u, (lo, hi) = i // 3, PIECES[i % 3]
+            nc.vector.tensor_copy(
+                gath[a][:, u, lo:hi].rearrange("p n e -> p (n e)").bitcast(U32),
+                pairs[a][:, u].rearrange("p w e -> p (w e)").bitcast(U32).indirect(offs_sb[:, lo // 16 : hi // 16]),
+            )
 
-        def cast(a, u):
-            if a == PASSES - 1:
-                nc.scalar.copy(planes[:, 2 * u : 2 * u + 2], raw[a][:, 2 * u : 2 * u + 2])
-                return
-            if u == 0:
-                pairs[a] = keep.tile([P, 2, T, 2], BF16, name=f"pairs_{a}", align_bytes=64)
-            src = raw[a][:, 2 * u : 2 * u + 2].rearrange("p e w -> p w e")
-            if a == 0 and u == 0:
-                nc.vector.tensor_copy(pairs[a][:, u], src)
-            else:
-                nc.scalar.copy(pairs[a][:, u], src)
+        def interleave(a):
+            nc.vector.tensor_copy(
+                q_in[a][:].rearrange("p n (u e) -> p n u e", u=2), gath[a][:].rearrange("p u n e -> p n u e")
+            )
 
-        banks = [psum.tile([P, N], F32, name=f"bank{i}", tag=f"bank{i}") for i in range(8)]
-        codes = {}
-        scales = {}
-        def new_codes(a):
-            codes[a] = keep.tile([P, SLOTS], U32, name=f"codes_{a}", align_bytes=64)
-            scales[a] = keep.tile([P, SLOTS], U8, name=f"scales_{a}", align_bytes=64)
+        def quantize(a, lo, hi):
+            nc.vector.quantize_mx(
+                out=codes[a][:, lo:hi].bitcast(FP8X4),
+                scales=scales[a][:, lo:hi],
+                in_=q_in[a][:, lo:hi].rearrange("p n t -> p (n t)"),
+            )
 
-        def vector_pass(a):
-            gath = keep.tile([P, 2, SLOTS, 2], BF16, name=f"gath_{a}", align_bytes=64)
-            q_in = keep.tile([P, SLOTS, 2, 2], BF16, name=f"q_in_{a}", align_bytes=64)
-            new_codes(a)
-            for u in range(2):
-                for lo, hi in ((0, 384), (384, 768), (768, 1024)):
-                    nc.vector.tensor_copy(
-                        gath[:, u, lo:hi].rearrange("p n e -> p (n e)").bitcast(U32),
-                        pairs[a][:, u].rearrange("p w e -> p (w e)").bitcast(U32).indirect(offs_sb[:, lo // 16 : hi // 16]),
-                    )
-            nc.vector.tensor_copy(q_in[:], gath[:].rearrange("p u n e -> p n u e"))
-            nc.vector.quantize_mx(out=codes[a][:].bitcast(FP8X4), scales=scales[a][:], in_=q_in[:].rearrange("p n u e -> p (n u e)"))
-
-        def scalar_chunk(a, e):
-            q_in = keep.tile([P, C, 4], BF16, name=f"q_in_{a}_{e}", align_bytes=64)
+        def scalar_gather(e):
             for t in range(4):
-                nc.scalar.activation(q_in[:, :, t], planes[:, t].indirect(offs_sb[:, e * C // 16 : (e + 1) * C // 16]), COPY)
-            cols = slice(e * C, (e + 1) * C)
-            nc.vector.quantize_mx(out=codes[a][:, cols].bitcast(FP8X4), scales=scales[a][:, cols], in_=q_in[:].rearrange("p n t -> p (n t)"))
+                nc.scalar.activation(
+                    q_in[LAST][:, e * C : (e + 1) * C, t],
+                    planes[:, t].indirect(offs_sb[:, e * C // 16 : (e + 1) * C // 16]),
+                    COPY,
+                )
 
         def multiply(a, e):
             for h in range(2):
@@ -111,60 +108,94 @@ def tile_moe_shr_lin_relu_kernel(tc, xT, w_words, w_scales, b, gate, offs, pos1,
                     rhs=codes[a][:, cols].bitcast(FP8X4),
                     rhs_scale=scales[a][:, cols],
                     start=(a == 0),
-                    stop=(a == PASSES - 1),
+                    stop=(a == LAST),
                 )
 
-        cast(0, 0)
-        cast(0, 1)
+        s_in, s_codes, s_scales = {}, {}, {}
         for a in range(PASSES):
-            if a + 1 < PASSES:
-                cast(a + 1, 0)
-                cast(a + 1, 1)
-            if a < PASSES - 1:
-                vector_pass(a)
-            else:
-                new_codes(a)
-            for e in range(E):
-                if a == PASSES - 1:
-                    scalar_chunk(a, e)
-                multiply(a, e)
-                if a == PASSES - 1:
-                    for h in range(2):
-                        nc.scalar.activation(
-                            y_sb[:, e * C + h * N : e * C + (h + 1) * N], banks[2 * e + h][:], RELU, bias=b_sb[:, e : e + 1]
-                        )
+            s_in[a] = keep.tile([P, T, 4], BF16, name=f"s_in_{a}", align_bytes=64)
+            s_codes[a] = keep.tile([P, T], U32, name=f"s_codes_{a}", align_bytes=64)
+            s_scales[a] = keep.tile([P, T], U8, name=f"s_scales_{a}", align_bytes=64)
 
+        def shared_interleave(a):
+            if a == LAST:
+                nc.scalar.copy(s_in[a][:], raw[a][:].rearrange("p t w -> p w t"))
+            else:
+                nc.vector.tensor_copy(
+                    s_in[a][:].rearrange("p n (u e) -> p n u e", u=2), pairs[a][:].rearrange("p u w e -> p w u e")
+                )
+
+        def shared_quantize(a):
+            nc.vector.quantize_mx(
+                out=s_codes[a][:].bitcast(FP8X4), scales=s_scales[a][:], in_=s_in[a][:].rearrange("p n t -> p (n t)")
+            )
+
+        cast(0, 0, 0, 320, nc.vector.tensor_copy)
+        cast(0, 0, 320, T, nc.scalar.copy)
+        cast(0, 1, 0, T, nc.scalar.copy)
+        for a in range(1, LAST):
+            for u in range(2):
+                cast(a, u, 0, T, nc.scalar.copy)
+        for u in range(2):
+            nc.scalar.copy(planes[:, 2 * u : 2 * u + 2], raw[LAST][:, 2 * u : 2 * u + 2])
+        for e in range(E):
+            scalar_gather(e)
+        for i in range(6):
+            gather(0, i)
+        for a in range(1, LAST):
+            gather(a, 0)
+            interleave(a - 1)
+            gather(a, 1)
+            quantize(a - 1, 0, SLOTS)
+            for e in range(E):
+                multiply(a - 1, e)
+            for i in range(2, 6):
+                gather(a, i)
+        shared_interleave(0)
+        interleave(LAST - 1)
+        shared_interleave(1)
+        quantize(LAST - 1, 0, SLOTS)
+        for e in range(E):
+            multiply(LAST - 1, e)
+        shared_interleave(2)
+        shared_quantize(0)
+        for e in range(E):
+            quantize(LAST, e * C, (e + 1) * C)
+            multiply(LAST, e)
+            for h in range(2):
+                nc.scalar.activation(
+                    y_sb[:, e * C + h * N : e * C + (h + 1) * N], banks[2 * e + h][:], RELU, bias=b_sb[:, e : e + 1]
+                )
+        shared_interleave(LAST)
         shared = psum.tile([P, T], F32, name="shared", tag="bank0")
         for a in range(PASSES):
-            q_in = keep.tile([P, T, 4], BF16, name=f"q_shared_{a}", align_bytes=64)
-            for lo in range(0, T, 64):
-                nc.gpsimd.tensor_scalar(
-                    q_in[:, lo : lo + 64], raw[a][:, :, lo : lo + 64].rearrange("p t w -> p w t"), 1.0, 0.0, MULT, ADD
-                )
-            s_codes = keep.tile([P, T], U32, name=f"s_codes_{a}", align_bytes=64)
-            s_scales = keep.tile([P, T], U8, name=f"s_scales_{a}", align_bytes=64)
-            nc.vector.quantize_mx(out=s_codes[:].bitcast(FP8X4), scales=s_scales[:], in_=q_in[:].rearrange("p n t -> p (n t)"))
+            if a:
+                shared_quantize(a)
             nc.tensor.matmul_mx(
                 out=shared[:],
                 lhsT=w_sb[:, E * PASSES + a, :].bitcast(FP4X4),
                 lhsT_scale=ws_sb[:, E * PASSES + a, :],
-                rhs=s_codes[:].bitcast(FP8X4),
-                rhs_scale=s_scales[:],
+                rhs=s_codes[a][:].bitcast(FP8X4),
+                rhs_scale=s_scales[a][:],
                 start=(a == 0),
-                stop=(a == PASSES - 1),
+                stop=(a == LAST),
             )
         nc.scalar.activation(ys_sb[:], shared[:], RELU, bias=b_sb[:, E : E + 1])
 
         half = T // 2
+        picked = {}
+        for r, lst in enumerate((pos1_sb, pos2_sb)):
+            for h in range(2):
+                cols = slice(h * half, (h + 1) * half)
+                picked[r, h] = keep.tile([P, half], F32, name=f"picked_{r}_{h}")
+                nc.vector.tensor_tensor(
+                    picked[r, h][:], y_sb[:].indirect(lst[:, h * half // 16 : (h + 1) * half // 16]), gate_sb[:, r, cols], MULT
+                )
+        partial = {}
         for h in range(2):
-            cols = slice(h * half, (h + 1) * half)
-            lst = slice(h * half // 16, (h + 1) * half // 16)
-            first = keep.tile([P, half], F32, name=f"first_{h}")
-            second = keep.tile([P, half], F32, name=f"second_{h}")
-            nc.vector.tensor_tensor(first[:], y_sb[:].indirect(pos1_sb[:, lst]), gate_sb[:, 0, cols], MULT)
-            nc.vector.tensor_tensor(second[:], y_sb[:].indirect(pos2_sb[:, lst]), gate_sb[:, 1, cols], MULT)
-            partial = keep.tile([P, half], F32, name=f"partial_{h}")
+            partial[h] = keep.tile([P, half], F32, name=f"partial_{h}")
+            nc.vector.tensor_add(partial[h][:], picked[0, h][:], ys_sb[:, h * half : (h + 1) * half])
+        for h in range(2):
             total = keep.tile([P, half], F32, name=f"total_{h}")
-            nc.vector.tensor_add(partial[:], first[:], ys_sb[:, cols])
-            nc.vector.tensor_add(total[:], partial[:], second[:])
-            nc.sync.dma_start(out[:, cols], total[:])
+            nc.vector.tensor_add(total[:], partial[h][:], picked[1, h][:])
+            nc.sync.dma_start(out[:, h * half : (h + 1) * half], total[:])

@@ -20,7 +20,7 @@ K_PASS = 512
 PASSES = K // K_PASS
 LAST = PASSES - 1
 SLOTS = E * C
-PIECES = ((0, 384), (384, 768), (768, 1024))
+PIECES = {1: ((0, 384), (384, 768), (768, 1024)), 2: ((0, 768), (768, 1024)), 3: ((0, 1024),)}
 
 FLOPS = 2 * K * N * (SLOTS + T)
 
@@ -42,23 +42,29 @@ def tile_moe_shr_lin_relu_kernel(tc, xT, w_words, w_scales, b, gate, offs, pos1,
         ys_sb = keep.tile([P, T], F32, name="ys_sb")
         planes = keep.tile([P, 4, T], BF16, name="planes", align_bytes=64)
         banks = [psum.tile([P, N], F32, name=f"bank{i}", tag=f"bank{i}") for i in range(8)]
-        raw, pairs, gath, q_in, codes, scales = {}, {}, {}, {}, {}, {}
+        first_pairs = keep.tile([P, 2, T, 2], BF16, name="first_pairs", align_bytes=64)
+        more_pairs = keep.tile([P, 4, T, 2], BF16, name="more_pairs", align_bytes=64)
+        pairs = {0: first_pairs[:], 1: more_pairs[:, 0:2], 2: more_pairs[:, 2:4]}
+        windows = {(0, 0): first_pairs[:, 0:1], (0, 1): first_pairs[:, 1:2]}
+        for s in range(4):
+            windows[1 + s // 2, s % 2] = more_pairs[:, s : min(s + 3, 4)]
+        raw, gath, q_in, codes, scales = {}, {}, {}, {}, {}
         for a in range(PASSES):
             raw[a] = keep.tile([P, 4, T], F32, name=f"raw_{a}")
             codes[a] = keep.tile([P, SLOTS], U32, name=f"codes_{a}", align_bytes=64)
             scales[a] = keep.tile([P, SLOTS], U8, name=f"scales_{a}", align_bytes=64)
             q_in[a] = keep.tile([P, SLOTS, 4], BF16, name=f"q_in_{a}", align_bytes=64)
             if a != LAST:
-                pairs[a] = keep.tile([P, 2, T, 2], BF16, name=f"pairs_{a}", align_bytes=64)
                 gath[a] = keep.tile([P, 2, SLOTS, 2], BF16, name=f"gath_{a}", align_bytes=64)
 
         nc.vector.memset(ws_sb[:].rearrange("p g n -> p (g n)").bitcast(I32), 0)
 
-        nc.sync.dma_start(offs_sb[:], offs)
         for a in range(PASSES):
             rows = xT[a * K_PASS : (a + 1) * K_PASS, :].rearrange("(p u e) w -> u p e w", u=2, e=2)
             for u in range(2):
                 nc.sync.dma_start(raw[a][:, 2 * u : 2 * u + 2], rows[u])
+                if a == 0 and u == 0:
+                    nc.sync.dma_start(offs_sb[:], offs)
         nc.sync.dma_start(w_sb[:].bitcast(I32), w_words.rearrange("e a p n -> p (e a) n").bitcast(I32))
         scale_rows = w_scales.rearrange("e a q n -> q (e a) n").bitcast(I32)
         for quad in range(4):
@@ -71,12 +77,13 @@ def tile_moe_shr_lin_relu_kernel(tc, xT, w_words, w_scales, b, gate, offs, pos1,
         def cast(a, u, lo, hi, copy):
             copy(pairs[a][:, u, lo:hi], raw[a][:, 2 * u : 2 * u + 2, lo:hi].rearrange("p e w -> p w e"))
 
-        def gather(a, i):
-            u, (lo, hi) = i // 3, PIECES[i % 3]
-            nc.vector.tensor_copy(
-                gath[a][:, u, lo:hi].rearrange("p n e -> p (n e)").bitcast(U32),
-                pairs[a][:, u].rearrange("p w e -> p (w e)").bitcast(U32).indirect(offs_sb[:, lo // 16 : hi // 16]),
-            )
+        def gather(a, u):
+            window = windows[a, u]
+            for lo, hi in PIECES[window.shape[1]]:
+                nc.vector.tensor_copy(
+                    gath[a][:, u, lo:hi].rearrange("p n e -> p (n e)").bitcast(U32),
+                    window.rearrange("p s w e -> p (s w e)").bitcast(U32).indirect(offs_sb[:, lo // 16 : hi // 16]),
+                )
 
         def interleave(a):
             nc.vector.tensor_copy(
@@ -122,7 +129,7 @@ def tile_moe_shr_lin_relu_kernel(tc, xT, w_words, w_scales, b, gate, offs, pos1,
                 nc.scalar.copy(s_in[a][:], raw[a][:].rearrange("p t w -> p w t"))
             else:
                 nc.vector.tensor_copy(
-                    s_in[a][:].rearrange("p n (u e) -> p n u e", u=2), pairs[a][:].rearrange("p u w e -> p w u e")
+                    s_in[a][:].rearrange("p n (u e) -> p n u e", u=2), pairs[a].rearrange("p u w e -> p w u e")
                 )
 
         def shared_quantize(a):
@@ -140,8 +147,8 @@ def tile_moe_shr_lin_relu_kernel(tc, xT, w_words, w_scales, b, gate, offs, pos1,
             nc.scalar.copy(planes[:, 2 * u : 2 * u + 2], raw[LAST][:, 2 * u : 2 * u + 2])
         for e in range(E):
             scalar_gather(e)
-        for i in range(6):
-            gather(0, i)
+        gather(0, 0)
+        gather(0, 1)
         for a in range(1, LAST):
             gather(a, 0)
             interleave(a - 1)
@@ -149,8 +156,6 @@ def tile_moe_shr_lin_relu_kernel(tc, xT, w_words, w_scales, b, gate, offs, pos1,
             quantize(a - 1, 0, SLOTS)
             for e in range(E):
                 multiply(a - 1, e)
-            for i in range(2, 6):
-                gather(a, i)
         shared_interleave(0)
         interleave(LAST - 1)
         shared_interleave(1)
@@ -160,7 +165,8 @@ def tile_moe_shr_lin_relu_kernel(tc, xT, w_words, w_scales, b, gate, offs, pos1,
         shared_interleave(2)
         shared_quantize(0)
         for e in range(E):
-            quantize(LAST, e * C, (e + 1) * C)
+            if e % 2 == 0:
+                quantize(LAST, e * C, (e + 2) * C)
             multiply(LAST, e)
             for h in range(2):
                 nc.scalar.activation(
@@ -183,19 +189,19 @@ def tile_moe_shr_lin_relu_kernel(tc, xT, w_words, w_scales, b, gate, offs, pos1,
         nc.scalar.activation(ys_sb[:], shared[:], RELU, bias=b_sb[:, E : E + 1])
 
         half = T // 2
-        picked = {}
-        for r, lst in enumerate((pos1_sb, pos2_sb)):
-            for h in range(2):
-                cols = slice(h * half, (h + 1) * half)
-                picked[r, h] = keep.tile([P, half], F32, name=f"picked_{r}_{h}")
-                nc.vector.tensor_tensor(
-                    picked[r, h][:], y_sb[:].indirect(lst[:, h * half // 16 : (h + 1) * half // 16]), gate_sb[:, r, cols], MULT
-                )
-        partial = {}
+        first = keep.tile([P, T], F32, name="first")
+        second = keep.tile([P, T], F32, name="second")
+        partial = keep.tile([P, T], F32, name="partial")
+        total = keep.tile([P, T], F32, name="total")
+
+        def pick(dst, r, lst, lo, hi):
+            nc.vector.tensor_tensor(dst[:, lo:hi], y_sb[:].indirect(lst[:, lo // 16 : hi // 16]), gate_sb[:, r, lo:hi], MULT)
+
+        pick(first, 0, pos1_sb, 0, T)
+        pick(second, 1, pos2_sb, 0, half)
+        nc.vector.tensor_add(partial[:], first[:], ys_sb[:])
+        pick(second, 1, pos2_sb, half, T)
         for h in range(2):
-            partial[h] = keep.tile([P, half], F32, name=f"partial_{h}")
-            nc.vector.tensor_add(partial[h][:], picked[0, h][:], ys_sb[:, h * half : (h + 1) * half])
-        for h in range(2):
-            total = keep.tile([P, half], F32, name=f"total_{h}")
-            nc.vector.tensor_add(total[:], partial[h][:], picked[1, h][:])
-            nc.sync.dma_start(out[:, h * half : (h + 1) * half], total[:])
+            cols = slice(h * half, (h + 1) * half)
+            nc.vector.tensor_add(total[:, cols], partial[:, cols], second[:, cols])
+            nc.sync.dma_start(out[:, cols], total[:, cols])

from contextlib import ExitStack

import concourse.mybir as mybir

F32 = mybir.dt.float32
BF16 = mybir.dt.bfloat16
U32 = mybir.dt.uint32
I32 = mybir.dt.int32
U16 = mybir.dt.uint16
U8 = mybir.dt.uint8
FP8X4 = mybir.dt.float8_e4m3fn_x4
FP4X4 = mybir.dt.float4_e2m1fn_x4
RELU = mybir.ActivationFunctionType.Relu
COPY = mybir.ActivationFunctionType.Copy
MULT = mybir.AluOpType.mult

P = 128
K, T, E, C, N = 2048, 512, 4, 256, 128
K_PASS = 512
PASSES = K // K_PASS
LAST = PASSES - 1
SLOTS = E * C
PIECES = {1: ((0, 384), (384, 768), (768, 1024)), 2: ((0, 768), (768, 1024)), 3: ((0, 1024),)}

FLOPS = 2 * K * N * (SLOTS + T)


def tile_moe_shr_lin_relu_kernel(tc, xT, w_words, w_scales, b, gate, offs, pos1, pos2, out):
    nc = tc.nc
    with ExitStack() as ctx:
        keep = ctx.enter_context(tc.tile_pool(name="keep", bufs=1))
        psum = ctx.enter_context(tc.psum_pool(name="psum", bufs=1))

        offs_sb = keep.tile([P, SLOTS // 16], U16, name="offs_sb")
        pos1_sb = keep.tile([P, T // 16], U16, name="pos1_sb")
        pos2_sb = keep.tile([P, T // 16], U16, name="pos2_sb")
        w_sb = keep.tile([P, (E + 1) * PASSES, 2 * N], U8, name="w_sb", align_bytes=64)
        ws_sb = keep.tile([P, (E + 1) * PASSES, N], U8, name="ws_sb", align_bytes=64)
        b_sb = keep.tile([P, E + 1], F32, name="b_sb")
        gate_sb = keep.tile([P, 2, T], F32, name="gate_sb")
        y_sb = keep.tile([P, SLOTS], F32, name="y_sb")
        ys_sb = keep.tile([P, T], F32, name="ys_sb")
        planes = keep.tile([P, 4, T], BF16, name="planes", align_bytes=64)
        banks = [psum.tile([P, N], F32, name=f"bank{i}", tag=f"bank{i}") for i in range(8)]
        first_pairs = keep.tile([P, 2, T, 2], BF16, name="first_pairs", align_bytes=64)
        more_pairs = keep.tile([P, 4, T, 2], BF16, name="more_pairs", align_bytes=64)
        pairs = {0: first_pairs[:], 1: more_pairs[:, 0:2], 2: more_pairs[:, 2:4]}
        windows = {(0, 0): first_pairs[:, 0:1], (0, 1): first_pairs[:, 1:2]}
        for s in range(4):
            windows[1 + s // 2, s % 2] = more_pairs[:, s : min(s + 3, 4)]
        raw, gath, q_in, codes, scales = {}, {}, {}, {}, {}
        for a in range(PASSES):
            raw[a] = keep.tile([P, 4, T], F32, name=f"raw_{a}")
            codes[a] = keep.tile([P, SLOTS], U32, name=f"codes_{a}", align_bytes=64)
            scales[a] = keep.tile([P, SLOTS], U8, name=f"scales_{a}", align_bytes=64)
            q_in[a] = keep.tile([P, SLOTS, 4], BF16, name=f"q_in_{a}", align_bytes=64)
            if a != LAST:
                gath[a] = keep.tile([P, 2, SLOTS, 2], BF16, name=f"gath_{a}", align_bytes=64)

        nc.vector.memset(ws_sb[:].rearrange("p g n -> p (g n)").bitcast(I32), 0)

        for a in range(PASSES):
            rows = xT[a * K_PASS : (a + 1) * K_PASS, :].rearrange("(p u e) w -> u p e w", u=2, e=2)
            for u in range(2):
                nc.sync.dma_start(raw[a][:, 2 * u : 2 * u + 2], rows[u])
                if a == 0 and u == 0:
                    nc.sync.dma_start(offs_sb[:], offs)
        nc.sync.dma_start(w_sb[:].bitcast(I32), w_words.rearrange("e a p n -> p (e a) n").bitcast(I32))
        scale_rows = w_scales.rearrange("e a q n -> q (e a) n").bitcast(I32)
        for quad in range(4):
            nc.sync.dma_start(ws_sb[32 * quad : 32 * quad + 4].bitcast(I32), scale_rows[4 * quad : 4 * quad + 4])
        nc.sync.dma_start(b_sb[:], b)
        nc.sync.dma_start(pos1_sb[:], pos1)
        nc.sync.dma_start(pos2_sb[:], pos2)
        nc.sync.dma_start(gate_sb[:], gate.rearrange("r n t -> n r t"))

        def cast(a, u, lo, hi, copy):
            copy(pairs[a][:, u, lo:hi], raw[a][:, 2 * u : 2 * u + 2, lo:hi].rearrange("p e w -> p w e"))

        def gather(a, u):
            window = windows[a, u]
            for lo, hi in PIECES[window.shape[1]]:
                nc.vector.tensor_copy(
                    gath[a][:, u, lo:hi].rearrange("p n e -> p (n e)").bitcast(U32),
                    window.rearrange("p s w e -> p (s w e)").bitcast(U32).indirect(offs_sb[:, lo // 16 : hi // 16]),
                )

        def interleave(a):
            nc.vector.tensor_copy(
                q_in[a][:].rearrange("p n (u e) -> p n u e", u=2), gath[a][:].rearrange("p u n e -> p n u e")
            )

        def quantize(a, lo, hi):
            nc.vector.quantize_mx(
                out=codes[a][:, lo:hi].bitcast(FP8X4),
                scales=scales[a][:, lo:hi],
                in_=q_in[a][:, lo:hi].rearrange("p n t -> p (n t)"),
            )

        def scalar_gather(e):
            for t in range(4):
                nc.scalar.activation(
                    q_in[LAST][:, e * C : (e + 1) * C, t],
                    planes[:, t].indirect(offs_sb[:, e * C // 16 : (e + 1) * C // 16]),
                    COPY,
                )

        def multiply(a, e):
            for h in range(2):
                cols = slice(e * C + h * N, e * C + (h + 1) * N)
                nc.tensor.matmul_mx(
                    out=banks[2 * e + h][:],
                    lhsT=w_sb[:, e * PASSES + a, :].bitcast(FP4X4),
                    lhsT_scale=ws_sb[:, e * PASSES + a, :],
                    rhs=codes[a][:, cols].bitcast(FP8X4),
                    rhs_scale=scales[a][:, cols],
                    start=(a == 0),
                    stop=(a == LAST),
                )

        s_in, s_codes, s_scales = {}, {}, {}
        for a in range(PASSES):
            s_in[a] = keep.tile([P, T, 4], BF16, name=f"s_in_{a}", align_bytes=64)
            s_codes[a] = keep.tile([P, T], U32, name=f"s_codes_{a}", align_bytes=64)
            s_scales[a] = keep.tile([P, T], U8, name=f"s_scales_{a}", align_bytes=64)

        def shared_interleave(a):
            if a == LAST:
                nc.scalar.copy(s_in[a][:], raw[a][:].rearrange("p t w -> p w t"))
            else:
                nc.vector.tensor_copy(
                    s_in[a][:].rearrange("p n (u e) -> p n u e", u=2), pairs[a].rearrange("p u w e -> p w u e")
                )

        def shared_quantize(a):
            nc.vector.quantize_mx(
                out=s_codes[a][:].bitcast(FP8X4), scales=s_scales[a][:], in_=s_in[a][:].rearrange("p n t -> p (n t)")
            )

        cast(0, 0, 0, 320, nc.vector.tensor_copy)
        cast(0, 0, 320, T, nc.scalar.copy)
        cast(0, 1, 0, T, nc.scalar.copy)
        for a in range(1, LAST):
            for u in range(2):
                cast(a, u, 0, T, nc.scalar.copy)
        for u in range(2):
            nc.scalar.copy(planes[:, 2 * u : 2 * u + 2], raw[LAST][:, 2 * u : 2 * u + 2])
        for e in range(E):
            scalar_gather(e)
        gather(0, 0)
        gather(0, 1)
        for a in range(1, LAST):
            gather(a, 0)
            interleave(a - 1)
            gather(a, 1)
            quantize(a - 1, 0, SLOTS)
            for e in range(E):
                multiply(a - 1, e)
        shared_interleave(0)
        interleave(LAST - 1)
        shared_interleave(1)
        quantize(LAST - 1, 0, SLOTS)
        for e in range(E):
            multiply(LAST - 1, e)
        shared_interleave(2)
        shared_quantize(0)
        for e in range(E):
            if e % 2 == 0:
                quantize(LAST, e * C, (e + 2) * C)
            multiply(LAST, e)
            for h in range(2):
                nc.scalar.activation(
                    y_sb[:, e * C + h * N : e * C + (h + 1) * N], banks[2 * e + h][:], RELU, bias=b_sb[:, e : e + 1]
                )
        shared_interleave(LAST)
        shared = psum.tile([P, T], F32, name="shared", tag="bank0")
        for a in range(PASSES):
            if a:
                shared_quantize(a)
            nc.tensor.matmul_mx(
                out=shared[:],
                lhsT=w_sb[:, E * PASSES + a, :].bitcast(FP4X4),
                lhsT_scale=ws_sb[:, E * PASSES + a, :],
                rhs=s_codes[a][:].bitcast(FP8X4),
                rhs_scale=s_scales[a][:],
                start=(a == 0),
                stop=(a == LAST),
            )
        nc.scalar.activation(ys_sb[:], shared[:], RELU, bias=b_sb[:, E : E + 1])

        half = T // 2
        first = keep.tile([P, T], F32, name="first")
        second = keep.tile([P, T], F32, name="second")
        partial = keep.tile([P, T], F32, name="partial")
        total = keep.tile([P, T], F32, name="total")

        def pick(dst, r, lst, lo, hi):
            nc.vector.tensor_tensor(dst[:, lo:hi], y_sb[:].indirect(lst[:, lo // 16 : hi // 16]), gate_sb[:, r, lo:hi], MULT)

        pick(first, 0, pos1_sb, 0, T)
        pick(second, 1, pos2_sb, 0, half)
        nc.vector.tensor_add(partial[:], first[:], ys_sb[:])
        pick(second, 1, pos2_sb, half, T)
        for h in range(2):
            cols = slice(h * half, (h + 1) * half)
            nc.vector.tensor_add(total[:, cols], partial[:, cols], second[:, cols])
            nc.sync.dma_start(out[:, cols], total[:, cols])
